import numpy as np
import ml_dtypes


def mxq(x, axis, fmt="e4m3"):
    dtype, down = {"e4m3": (ml_dtypes.float8_e4m3fn, 7), "e5m2": (ml_dtypes.float8_e5m2, 14)}[fmt]
    v = np.moveaxis(np.asarray(x, np.float32).astype(ml_dtypes.bfloat16).astype(np.float64), axis, -1)
    blocks = v.reshape(v.shape[:-1] + (-1, 32))
    amax = np.abs(blocks).max(-1, keepdims=True)
    byte = np.maximum(np.where(amax > 0, np.frexp(amax)[1] - 1 + 127, 0) - down, 1)
    scale = np.exp2(byte - 127.0)
    codes = (blocks / scale).astype(np.float32).astype(dtype).astype(np.float64)
    return np.moveaxis((codes * scale).reshape(v.shape), -1, axis)


WIDE = False


def mx_kscale(k):
    if not WIDE:
        return np.ones(k)
    levels = np.array([10, -10, 5, -5, 0])
    if k % 512:
        return np.exp2(np.random.permutation(np.resize(levels, k // 32))).repeat(32)
    a = np.empty((k // 512, 16))
    for p in range(k // 512):
        a[p, :8] = np.random.permutation(np.resize(levels, 8))
        for g in range(8):
            far = levels[np.abs(levels - a[p, g]) >= 10]
            a[p, g + 8] = far[np.random.randint(len(far))]
    return np.exp2(a.ravel()).repeat(32)


def f64(x):
    return np.asarray(x).astype(np.float64)


def striped(idx):
    return np.tile(idx.reshape(-1, 16).T, (8, 1)).astype(np.uint16)


def unstriped(offs):
    return offs[:16].T.reshape(-1).astype(np.int64)


E2M1 = np.array([0.0, 0.5, 1.0, 1.5, 2.0, 3.0, 4.0, 6.0, -0.0, -0.5, -1.0, -1.5, -2.0, -3.0, -4.0, -6.0])


def pack_weight(w, fmt):
    k, n = w.shape
    w = f64(np.asarray(w, np.float32).astype(ml_dtypes.bfloat16)).reshape(k // 32, 32, n)
    amax = np.abs(w).max(1)
    if fmt == "e4m3":
        byte = np.frexp(amax)[1] - 1 + 127 - 7
    else:
        mant, ex = np.frexp(amax / 6.0)
        byte = np.where(mant > 0.5, ex, ex - 1) + 127
    byte = np.clip(np.where(amax > 0, byte, 1), 1, 254)
    scaled = (w * np.exp2(127.0 - byte)[:, None, :]).reshape(k, n).astype(np.float32)
    by_word = np.ascontiguousarray(scaled.reshape(k // 512, 128, 4, n).transpose(0, 1, 3, 2))
    if fmt == "e4m3":
        words = by_word.astype(ml_dtypes.float8_e4m3fn).view(np.uint8)
    else:
        c = by_word.astype(ml_dtypes.float4_e2m1fn).view(np.uint8) & 0xF
        words = (c[..., 0::2] | (c[..., 1::2] << 4)).reshape(k // 512, 128, 2 * n)
    return np.ascontiguousarray(words), np.ascontiguousarray(byte.astype(np.uint8).reshape(k // 512, 16, n))


def unpack_weight(words, scales, fmt):
    g, _, n = scales.shape
    words = np.ascontiguousarray(words).reshape(g, 128, n, -1)
    if fmt == "e4m3":
        vals = words.view(ml_dtypes.float8_e4m3fn).astype(np.float64)
    else:
        nib = np.empty((g, 128, n, 4), np.uint8)
        nib[..., 0::2] = words & 0xF
        nib[..., 1::2] = words >> 4
        vals = E2M1[nib]
    vals = vals * np.repeat(np.exp2(scales.astype(np.float64) - 127.0), 8, axis=1)[..., None]
    return vals.transpose(0, 1, 3, 2).reshape(g * 512, n)


def gelu(v):
    return 0.5 * v * (1.0 + np.tanh(np.sqrt(2.0 / np.pi) * (v + 0.044715 * v**3)))


def striped8(idx):
    return np.concatenate([v.reshape(-1, 16).T for v in idx]).astype(np.uint16)


def unstriped8(offs):
    return np.stack([offs[16 * g:16 * g + 16].T.reshape(-1) for g in range(8)]).astype(np.int64)


def heads(h, wgt, idx8):
    r = np.arange(h.shape[0])
    return wgt[r // 4 % 128] * h[r[:, None], idx8[r % 512 // 64]]


def put_heads(h, wgs, idx8, t2):
    r = np.arange(h.shape[0])
    page = np.zeros((h.shape[0], t2))
    page[r[:, None], idx8[r % 512 // 64]] = wgs[r // 4 % 128] * h
    return page


K, T, S, P, T2, H, N = 512, 4096, 1024, 1024, 2048, 1536, 768


def setup_inputs():
    n = np.random.standard_normal
    s = mx_kscale(K)[:, None]
    u = mx_kscale(H)[:, None]
    d = {}
    d["tab_words"], d["tab_scales"] = pack_weight(n((K, T)) * s, "e4m3")
    d["offs"] = striped(np.random.permutation(T)[:S])
    d["offs2"] = striped8(np.stack([np.random.permutation(T2)[:S] for _ in range(8)]))
    d["offs3"] = striped8(np.stack([np.random.permutation(T2)[:P] for _ in range(8)]))
    d["wa_words"], d["wa_scales"] = pack_weight(1.6 * n((K, H)) / K**0.5 / s * u.T, "e2m1")
    d["wb"] = (1.3 * n((K, H)) / K**0.5 / s * u.T).astype(np.float32)
    d["unit"] = (np.exp(0.3 * n(H)) * u[:, 0]**2).astype(np.float32)
    d["wgs"] = np.repeat(np.random.uniform(0.5, 2.0, (8, S)), 16, axis=0).astype(np.float32)
    d["wgt"] = np.repeat(np.random.uniform(0.5, 2.0, (8, P)), 16, axis=0).astype(np.float32)
    d["clay"] = (1.5 * n((H, P)) * u).astype(np.float32)
    d["wo"] = (0.5 * n((H, N)) / H**0.5 / u).astype(np.float32)
    d["target"] = n((N, P)).astype(np.float32)
    return d


def reference(tab_words, tab_scales, offs, offs2, offs3, wa_words, wa_scales, wb, unit, wgs, wgt, clay, wo, target):
    v = unpack_weight(tab_words, tab_scales, "e4m3")[:, unstriped(offs)]
    a = unpack_weight(wa_words, wa_scales, "e2m1").T @ v
    b = mxq(f64(wb), 0, "e4m3").T @ v
    h = np.sqrt(np.square(a) + np.square(b) + f64(unit)[:, None])
    page = put_heads(h, f64(wgs), unstriped8(offs2), T2)
    x = heads(page, f64(wgt), unstriped8(offs3))
    z = mxq(x - f64(clay), 0, "e4m3")
    y = mxq(f64(wo), 0, "e4m3").T @ z
    return y - f64(target)

@@ -1,0 +1,314 @@
+from contextlib import ExitStack
+
+import concourse.mybir as mybir
+from concourse.masks import make_identity
+
+K, T, S, M, T2, H, N = 512, 4096, 1024, 1024, 2048, 1536, 768
+FLOPS = 2 * (2 * K * H * S + H * N * M)
+
+F32 = mybir.dt.float32
+BF16 = mybir.dt.bfloat16
+I32 = mybir.dt.int32
+U32 = mybir.dt.uint32
+U16 = mybir.dt.uint16
+U8 = mybir.dt.uint8
+FP8X4 = mybir.dt.float8_e4m3fn_x4
+FP4X4 = mybir.dt.float4_e2m1fn_x4
+ACT = mybir.ActivationFunctionType
+ALU = mybir.AluOpType
+
+P = 128
+PACK = 4
+R_PASS = P * PACK
+PASSES = H // R_PASS
+BANK = 512
+CHUNK = 256
+CHUNKS = M // CHUNK
+PIECE = 256
+N_TILES = N // P
+
+
+def tile_list_glaze_firing_deviation_kernel(
+    tc, tab_words, tab_scales, offs, offs2, offs3, wa_words, wa_scales, wb, unit, wgs, wgt, clay, wo, target, out
+):
+    nc = tc.nc
+    with ExitStack() as ctx:
+        sb = ctx.enter_context(tc.tile_pool(name="sb", bufs=1))
+        ps = ctx.enter_context(tc.psum_pool(name="ps", bufs=1))
+
+        def tile(name, cols, dtype):
+            return sb.tile([P, cols], dtype, name=name, align_bytes=64)
+
+        pick = tile("pick", S // 16, U16)
+        put = tile("put", S // 16, U16)
+        read = tile("read", M // 16, U16)
+        table = tile("table", T, U32)
+        table_scales = tile("table_scales", T, U8)
+        v_words = [tile("v_words%d" % half, BANK, U32) for half in range(2)]
+        v_scales = tile("v_scales", S, U8)
+        wa_codes = tile("wa_codes", 2 * H, U8)
+        wa_plane = tile("wa_plane", H, U8)
+        wb_raw = tile("wb_raw", PACK * R_PASS, F32)
+        wb_codes = [tile("wb_codes%d" % b, R_PASS, U32) for b in range(PASSES)]
+        wb_plane = [tile("wb_plane%d" % b, R_PASS, U8) for b in range(PASSES)]
+        wo_raw = tile("wo_raw", PACK * N, F32)
+        wo_codes = [tile("wo_codes%d" % b, N, U32) for b in range(PASSES)]
+        wo_plane = [tile("wo_plane%d" % b, N, U8) for b in range(PASSES)]
+        unit_cols = tile("unit_cols", PASSES * PACK, F32)
+        wgs_sb = tile("wgs_sb", S, F32)
+        wgt_neg = tile("wgt_neg", M, F32)
+        pages = [tile("page%d" % i, T2, F32) for i in range(PACK)]
+        squares = tile("squares", 8 * BANK, F32)
+        h_sb = [[tile("h%d_%d" % (half, i), BANK, F32) for i in range(PACK)] for half in range(2)]
+        x_neg = [tile("x_neg%d" % i, M, F32) for i in range(PACK)]
+        clay_sb = tile("clay_sb", PACK * M, F32)
+        z_turned = [tile("z_turned%d" % k, R_PASS, BF16) for k in range(4)]
+        z_rounded = [tile("z_rounded%d" % c, PACK * CHUNK, BF16) for c in range(CHUNKS)]
+        z_codes = [[tile("z_codes%d_%d" % (b, c), CHUNK, U32) for c in range(CHUNKS)] for b in range(PASSES)]
+        z_plane = [[tile("z_plane%d_%d" % (b, c), CHUNK, U8) for c in range(CHUNKS)] for b in range(PASSES)]
+        ident = tile("ident", P, F32)
+        warm = tile("warm", 8, F32)
+        width = N_TILES * CHUNK
+        result = [squares[:, 0:width], squares[:, width : 2 * width], wb_raw[:, 0:width], wo_raw[:, 0:width]]
+
+        banks = [ps.tile([P, BANK], F32, name="bank%d" % k) for k in range(8)]
+        ring = {"order": list(range(8)), "at": 0, "turned": 0}
+
+        def take_bank():
+            order = ring["order"]
+            bank = banks[order[ring["at"] % len(order)]]
+            ring["at"] = ring["at"] + 1
+            return bank
+
+        def load_scale_rows(plane, rows):
+            for quadrant in range(4):
+                nc.sync.dma_start(
+                    plane[32 * quadrant : 32 * quadrant + 4, :].bitcast(I32),
+                    rows[0, 4 * quadrant : 4 * quadrant + 4, :].bitcast(I32),
+                )
+
+        def load_wb(b):
+            nc.sync.dma_start(
+                wb_raw[:].rearrange("p (t c) -> p t c", t=PACK),
+                wb[:, b * R_PASS : (b + 1) * R_PASS].rearrange("(p t) c -> p t c", t=PACK),
+            )
+
+        def load_wo(b):
+            nc.sync.dma_start(wo_raw[:], wo[b * R_PASS : (b + 1) * R_PASS, :].rearrange("(p t) n -> p (t n)", t=PACK))
+
+        def load_clay(b):
+            nc.sync.dma_start(clay_sb[:], clay[b * R_PASS : (b + 1) * R_PASS, :].rearrange("(p t) m -> p (t m)", t=PACK))
+
+        def quantize_piece(name, raw, codes, plane, piece):
+            cols = slice(piece * PIECE, (piece + 1) * PIECE)
+            rounded = tile("%s_rounded%d" % (name, piece), PACK * PIECE, BF16)
+            nc.scalar.copy(
+                rounded[:].rearrange("p (c e t) -> p c t e", e=4, t=PACK),
+                raw[:].rearrange("p (t c) -> p t c", t=PACK)[:, :, cols].rearrange("p t (c e) -> p c t e", e=4),
+            )
+            nc.vector.quantize_mx(out=codes[:, cols].bitcast(FP8X4), scales=plane[:, cols], in_=rounded[:])
+
+        def quantize_wb(b, piece):
+            quantize_piece("wb%d" % b, wb_raw, wb_codes[b], wb_plane[b], piece)
+
+        def quantize_wo(b):
+            for piece in range(N // PIECE):
+                quantize_piece("wo%d" % b, wo_raw, wo_codes[b], wo_plane[b], piece)
+
+        def square_products(b, blocks):
+            for jb in blocks:
+                lhsT = v_words[jb // 4][:, (jb % 4) * P : (jb % 4 + 1) * P].bitcast(FP8X4)
+                lhsT_scale = v_scales[:, jb * P : (jb + 1) * P]
+                operands = (
+                    (wa_codes[:, 2 * b * R_PASS : 2 * (b + 1) * R_PASS].bitcast(FP4X4), wa_plane[:, b * R_PASS : (b + 1) * R_PASS]),
+                    (wb_codes[b][:].bitcast(FP8X4), wb_plane[b][:]),
+                )
+                for which, (rhs, rhs_scale) in enumerate(operands):
+                    bank = take_bank()
+                    nc.tensor.matmul_mx(bank[:], lhsT=lhsT, lhsT_scale=lhsT_scale, rhs=rhs, rhs_scale=rhs_scale, start=True, stop=True)
+                    at = (2 * (jb % 4) + which) * BANK
+                    nc.scalar.activation(
+                        squares[:, at : at + BANK].rearrange("p (i q) -> p i q", i=PACK),
+                        bank[:].rearrange("p (q i) -> p i q", i=PACK),
+                        ACT.Square,
+                    )
+
+        def root_and_put(b, blocks, slices):
+            count = len(blocks) * P
+            first = blocks[0] * P
+            bank = take_bank()
+            for place, i in enumerate(slices):
+                for step, jb in enumerate(blocks):
+                    at = place * count + step * P
+                    for which in range(2):
+                        src = (2 * (jb % 4) + which) * BANK + i * P
+                        nc.tensor.matmul(
+                            bank[:, at : at + P], lhsT=squares[:, src : src + P], rhs=ident[:],
+                            is_transpose=True, start=(which == 0), stop=(which == 1),
+                        )
+            for place, i in enumerate(slices):
+                h = h_sb[first // BANK][i][:, first % BANK : first % BANK + count]
+                nc.scalar.activation(
+                    h, bank[:, place * count : (place + 1) * count], ACT.Sqrt,
+                    bias=unit_cols[:, b * PACK + i : b * PACK + i + 1],
+                )
+                nc.vector.tensor_tensor(
+                    pages[i][:].indirect(put[:, first // 16 : (first + count) // 16]), h, wgs_sb[:, first : first + count], ALU.mult
+                )
+
+        def roots(b, blocks):
+            per_bank = BANK // (len(blocks) * P)
+            for i0 in range(0, PACK, per_bank):
+                root_and_put(b, blocks, list(range(i0, i0 + per_bank)))
+
+        def read_pages(first, count):
+            for i in range(PACK):
+                nc.vector.tensor_tensor(
+                    x_neg[i][:, first : first + count],
+                    pages[i][:].indirect(read[:, first // 16 : (first + count) // 16]),
+                    wgt_neg[:, first : first + count],
+                    ALU.mult,
+                )
+
+        def make_z(b, c):
+            turned = []
+            for block in range(CHUNK // P):
+                m0 = c * CHUNK + block * P
+                bank = take_bank()
+                for i in range(PACK):
+                    nc.tensor.matmul(
+                        bank[:, i * P : (i + 1) * P], lhsT=clay_sb[:, i * M + m0 : i * M + m0 + P], rhs=ident[:],
+                        is_transpose=True, start=(i == 0), stop=False,
+                    )
+                for i in range(PACK):
+                    nc.tensor.matmul(
+                        bank[:, i * P : (i + 1) * P], lhsT=x_neg[i][:, m0 : m0 + P], rhs=ident[:],
+                        is_transpose=True, start=False, stop=(i == PACK - 1),
+                    )
+                pairs = z_turned[ring["turned"] % len(z_turned)]
+                ring["turned"] = ring["turned"] + 1
+                nc.scalar.activation(
+                    pairs[:].rearrange("m (u p e) -> m u p e", u=2, e=2),
+                    bank[:].rearrange("m (u e p) -> m u p e", u=2, e=2),
+                    ACT.Copy,
+                    scale=-1.0,
+                )
+                turned.append(pairs)
+            bank = take_bank()
+            for block, pairs in enumerate(turned):
+                words = pairs[:].bitcast(F32)
+                for u in range(2):
+                    at = (2 * block + u) * P
+                    nc.tensor.transpose(bank[:, at : at + P], words[:, u * P : (u + 1) * P], ident[:])
+            nc.scalar.copy(
+                z_rounded[c][:].bitcast(F32).rearrange("p (k m u) -> p k m u", k=CHUNK // P, u=2),
+                bank[:].rearrange("p (k u m) -> p k m u", k=CHUNK // P, u=2),
+            )
+            nc.vector.quantize_mx(out=z_codes[b][c][:].bitcast(FP8X4), scales=z_plane[b][c][:], in_=z_rounded[c][:])
+
+        def score_passes(c, passes):
+            for pair in range(N_TILES // 2):
+                bank = banks[3 * (c % 2) + pair]
+                for b in passes:
+                    for side in range(2):
+                        cols = slice((2 * pair + side) * P, (2 * pair + side + 1) * P)
+                        nc.tensor.matmul_mx(
+                            bank[:, side * CHUNK : (side + 1) * CHUNK],
+                            lhsT=wo_codes[b][:, cols].bitcast(FP8X4), lhsT_scale=wo_plane[b][:, cols],
+                            rhs=z_codes[b][c][:].bitcast(FP8X4), rhs_scale=z_plane[b][c][:],
+                            start=(b == 0 and side == 0), stop=(b == PASSES - 1 and side == 1),
+                        )
+
+        def finish(c):
+            view = out.rearrange("(t p) m -> p t m", p=P)
+            for pair in range(N_TILES // 2):
+                bank = banks[3 * (c % 2) + pair]
+                part = result[c][:, pair * BANK : (pair + 1) * BANK]
+                nc.vector.tensor_tensor(part, bank[:], part, ALU.subtract)
+                nc.sync.dma_start(
+                    view[:, 2 * pair : 2 * pair + 2, c * CHUNK : (c + 1) * CHUNK], part.rearrange("p (t m) -> p t m", t=2)
+                )
+
+        def load_target(c):
+            nc.sync.dma_start(
+                result[c].rearrange("p (t m) -> p t m", t=N_TILES),
+                target.rearrange("(t p) m -> p t m", p=P)[:, :, c * CHUNK : (c + 1) * CHUNK],
+            )
+
+        nc.vector.memset(table_scales[:].bitcast(I32), 0)
+        nc.vector.memset(wa_plane[:].bitcast(I32), 0)
+        nc.vector.memset(warm[:], 1.0)
+        nc.scalar.activation(warm[:, 0:1], warm[:, 1:2], ACT.Sqrt)
+        make_identity(nc, ident[:])
+        load_wb(0)
+        load_scale_rows(table_scales, tab_scales)
+        nc.sync.dma_start(table[:].bitcast(I32), tab_words[0].rearrange("p t i -> p (t i)").bitcast(I32))
+        nc.sync.dma_start(pick[:], offs)
+        nc.sync.dma_start(wa_codes[:].bitcast(I32), wa_words[0].bitcast(I32))
+        load_scale_rows(wa_plane, wa_scales)
+        nc.sync.dma_start(
+            unit_cols[:].rearrange("p (b i) -> p b i", i=PACK), unit.rearrange("(b p i) -> p b i", p=P, i=PACK)
+        )
+        nc.sync.dma_start(wgs_sb[:], wgs)
+        nc.sync.dma_start(put[:], offs2)
+        nc.sync.dma_start(read[:], offs3)
+        for page in pages:
+            nc.vector.memset(page[:], 0.0)
+        for piece in range(2):
+            quantize_wb(0, piece)
+        load_clay(0)
+        load_wb(1)
+        nc.sync.dma_start(wgt_neg[:], wgt)
+        load_wo(0)
+        nc.vector.tensor_copy(v_scales[:], table_scales[:].indirect(pick[:]))
+        for half in range(2):
+            nc.vector.tensor_copy(v_words[half][:], table[:].indirect(pick[:, 32 * half : 32 * (half + 1)]))
+
+        low, high = [0, 1, 2, 3], [4, 5, 6, 7]
+        for blocks in ([0], [1], [2, 3]):
+            square_products(0, blocks)
+            roots(0, blocks)
+        square_products(0, high)
+        for i in range(PACK):
+            root_and_put(0, high, [i])
+            if i < 2:
+                quantize_wb(1, i)
+        load_wb(2)
+        nc.scalar.mul(wgt_neg[:], wgt_neg[:], -1.0)
+        read_pages(0, M)
+        quantize_wo(0)
+        load_wo(1)
+        square_products(1, low)
+        roots(1, low)
+        square_products(1, high)
+        for piece in range(2):
+            quantize_wb(2, piece)
+        load_target(2)
+        for c in range(CHUNKS):
+            make_z(0, c)
+        load_clay(1)
+        roots(1, high)
+        read_pages(0, M)
+        quantize_wo(1)
+        load_wo(2)
+        square_products(2, low)
+        roots(2, low)
+        square_products(2, high)
+        quantize_wo(2)
+        load_target(3)
+        for c in range(CHUNKS):
+            make_z(1, c)
+        load_clay(2)
+        roots(2, high)
+        load_target(0)
+        load_target(1)
+        ring["order"] = [6, 7]
+        for c in range(2):
+            score_passes(c, [0, 1])
+        for c in range(CHUNKS):
+            read_pages(c * CHUNK, CHUNK)
+            make_z(2, c)
+            if c >= 2:
+                score_passes(c, [0, 1])
+            score_passes(c, [2])
+            finish(c)

@@ -26,6 +26,7 @@ CHUNK = 256
 CHUNKS = M // CHUNK
 PIECE = 256
 N_TILES = N // P
+SCORE_BANKS = 5
 
 
 def tile_list_glaze_firing_deviation_kernel(
@@ -36,84 +37,88 @@ def tile_list_glaze_firing_deviation_kernel(
         sb = ctx.enter_context(tc.tile_pool(name="sb", bufs=1))
         ps = ctx.enter_context(tc.psum_pool(name="ps", bufs=1))
 
-        def tile(name, cols, dtype):
-            return sb.tile([P, cols], dtype, name=name, align_bytes=64)
+        def tile(name, cols, dtype, tag="", bufs=None):
+            return sb.tile([P, cols], dtype, name=name, tag=tag or name, bufs=bufs, align_bytes=64)
 
         pick = tile("pick", S // 16, U16)
         put = tile("put", S // 16, U16)
         read = tile("read", M // 16, U16)
-        table = tile("table", T, U32)
-        table_scales = tile("table_scales", T, U8)
+        table = tile("table", T, U32, tag="table_then_clay")
+        table_scales = tile("table_scales", T, U8, tag="scales_then_wgt")
         v_words = [tile("v_words%d" % half, BANK, U32) for half in range(2)]
         v_scales = tile("v_scales", S, U8)
         wa_codes = tile("wa_codes", 2 * H, U8)
         wa_plane = tile("wa_plane", H, U8)
-        wb_raw = tile("wb_raw", PACK * R_PASS, F32)
         wb_codes = [tile("wb_codes%d" % b, R_PASS, U32) for b in range(PASSES)]
         wb_plane = [tile("wb_plane%d" % b, R_PASS, U8) for b in range(PASSES)]
-        wo_raw = tile("wo_raw", PACK * N, F32)
         wo_codes = [tile("wo_codes%d" % b, N, U32) for b in range(PASSES)]
         wo_plane = [tile("wo_plane%d" % b, N, U8) for b in range(PASSES)]
         unit_cols = tile("unit_cols", PASSES * PACK, F32)
         wgs_sb = tile("wgs_sb", S, F32)
-        wgt_neg = tile("wgt_neg", M, F32)
         pages = [tile("page%d" % i, T2, F32) for i in range(PACK)]
-        squares = tile("squares", 8 * BANK, F32)
-        h_sb = [[tile("h%d_%d" % (half, i), BANK, F32) for i in range(PACK)] for half in range(2)]
-        x_neg = [tile("x_neg%d" % i, M, F32) for i in range(PACK)]
-        clay_sb = tile("clay_sb", PACK * M, F32)
+        squares = tile("squares", 8 * BANK, F32, tag="squares_then_result")
+        h_sb = [[tile("h%d_%d" % (side, i), S, F32) for i in range(PACK)] for side in range(2)]
+        x_neg = [tile("x_neg%d" % i, M, F32, tag="x_then_z%d" % i)[:] for i in range(PACK)]
         z_turned = [tile("z_turned%d" % k, R_PASS, BF16) for k in range(4)]
-        z_rounded = [tile("z_rounded%d" % c, PACK * CHUNK, BF16) for c in range(CHUNKS)]
-        z_codes = [[tile("z_codes%d_%d" % (b, c), CHUNK, U32) for c in range(CHUNKS)] for b in range(PASSES)]
-        z_plane = [[tile("z_plane%d_%d" % (b, c), CHUNK, U8) for c in range(CHUNKS)] for b in range(PASSES)]
+        z_whole = tile("z_whole", PACK * M, BF16, tag="z_then_x")
+        z_rounded = [z_whole[:, c * PACK * CHUNK : (c + 1) * PACK * CHUNK] for c in range(CHUNKS)]
+        z_codes = [tile("z_codes%d" % b, M, U32) for b in range(PASSES)]
+        z_plane = [tile("z_plane%d" % b, M, U8) for b in range(PASSES)]
         ident = tile("ident", P, F32)
         warm = tile("warm", 8, F32)
-        width = N_TILES * CHUNK
-        result = [squares[:, 0:width], squares[:, width : 2 * width], wb_raw[:, 0:width], wo_raw[:, 0:width]]
 
         banks = [ps.tile([P, BANK], F32, name="bank%d" % k) for k in range(8)]
-        ring = {"order": list(range(8)), "at": 0, "turned": 0}
+        ring = {"at": 0, "turned": 0}
 
         def take_bank():
-            order = ring["order"]
-            bank = banks[order[ring["at"] % len(order)]]
+            bank = banks[ring["at"] % len(banks)]
             ring["at"] = ring["at"] + 1
             return bank
 
-        def load_scale_rows(plane, rows):
+        def last_taken(count):
+            return [banks[(ring["at"] - count + k) % len(banks)] for k in range(count)]
+
+        def load_scale_rows(queue, plane, rows):
             for quadrant in range(4):
-                nc.sync.dma_start(
+                queue.dma_start(
                     plane[32 * quadrant : 32 * quadrant + 4, :].bitcast(I32),
                     rows[0, 4 * quadrant : 4 * quadrant + 4, :].bitcast(I32),
                 )
 
         def load_wb(b):
+            raw = tile("wb_raw%d" % b, PACK * R_PASS, F32, tag="raw_then_result")
             nc.sync.dma_start(
-                wb_raw[:].rearrange("p (t c) -> p t c", t=PACK),
+                raw[:].rearrange("p (t c) -> p t c", t=PACK),
                 wb[:, b * R_PASS : (b + 1) * R_PASS].rearrange("(p t) c -> p t c", t=PACK),
             )
+            return raw
 
         def load_wo(b):
-            nc.sync.dma_start(wo_raw[:], wo[b * R_PASS : (b + 1) * R_PASS, :].rearrange("(p t) n -> p (t n)", t=PACK))
+            raw = tile("wo_raw%d" % b, PACK * N, F32, tag="raw_then_result")
+            nc.sync.dma_start(raw[:], wo[b * R_PASS : (b + 1) * R_PASS, :].rearrange("(p t) n -> p (t n)", t=PACK))
+            return raw
 
         def load_clay(b):
+            clay_sb = tile("clay%d" % b, PACK * M, F32, tag="table_then_clay")
             nc.sync.dma_start(clay_sb[:], clay[b * R_PASS : (b + 1) * R_PASS, :].rearrange("(p t) m -> p (t m)", t=PACK))
+            return clay_sb
 
-        def quantize_piece(name, raw, codes, plane, piece):
-            cols = slice(piece * PIECE, (piece + 1) * PIECE)
-            rounded = tile("%s_rounded%d" % (name, piece), PACK * PIECE, BF16)
+        def quantize_columns(name, raw, codes, plane, first, count):
+            cols = slice(first, first + count)
+            rounded = tile("%s_rounded%d" % (name, first), PACK * count, BF16, tag="rounded", bufs=6)
             nc.scalar.copy(
                 rounded[:].rearrange("p (c e t) -> p c t e", e=4, t=PACK),
                 raw[:].rearrange("p (t c) -> p t c", t=PACK)[:, :, cols].rearrange("p t (c e) -> p c t e", e=4),
             )
             nc.vector.quantize_mx(out=codes[:, cols].bitcast(FP8X4), scales=plane[:, cols], in_=rounded[:])
 
-        def quantize_wb(b, piece):
-            quantize_piece("wb%d" % b, wb_raw, wb_codes[b], wb_plane[b], piece)
+        def quantize_wb(b, raw, width):
+            for first in range(0, R_PASS, width):
+                quantize_columns("wb%d" % b, raw, wb_codes[b], wb_plane[b], first, width)
 
-        def quantize_wo(b):
-            for piece in range(N // PIECE):
-                quantize_piece("wo%d" % b, wo_raw, wo_codes[b], wo_plane[b], piece)
+        def quantize_wo(b, raw):
+            quantize_columns("wo%d" % b, raw, wo_codes[b], wo_plane[b], 0, 512)
+            quantize_columns("wo%d" % b, raw, wo_codes[b], wo_plane[b], 512, 256)
 
         def square_products(b, blocks):
             for jb in blocks:
@@ -133,7 +138,15 @@ def tile_list_glaze_firing_deviation_kernel(
                         ACT.Square,
                     )
 
-        def root_and_put(b, blocks, slices):
+        def put_columns(b, i, first, count):
+            nc.vector.tensor_tensor(
+                pages[i][:].indirect(put[:, first // 16 : (first + count) // 16]),
+                h_sb[b % 2][i][:, first : first + count],
+                wgs_sb[:, first : first + count],
+                ALU.mult,
+            )
+
+        def root_slices(b, blocks, slices, put_now):
             count = len(blocks) * P
             first = blocks[0] * P
             bank = take_bank()
@@ -147,21 +160,20 @@ def tile_list_glaze_firing_deviation_kernel(
                             is_transpose=True, start=(which == 0), stop=(which == 1),
                         )
             for place, i in enumerate(slices):
-                h = h_sb[first // BANK][i][:, first % BANK : first % BANK + count]
+                h = h_sb[b % 2][i][:, first : first + count]
                 nc.scalar.activation(
                     h, bank[:, place * count : (place + 1) * count], ACT.Sqrt,
                     bias=unit_cols[:, b * PACK + i : b * PACK + i + 1],
                 )
-                nc.vector.tensor_tensor(
-                    pages[i][:].indirect(put[:, first // 16 : (first + count) // 16]), h, wgs_sb[:, first : first + count], ALU.mult
-                )
+                if put_now:
+                    put_columns(b, i, first, count)
 
-        def roots(b, blocks):
+        def roots(b, blocks, put_now):
             per_bank = BANK // (len(blocks) * P)
             for i0 in range(0, PACK, per_bank):
-                root_and_put(b, blocks, list(range(i0, i0 + per_bank)))
+                root_slices(b, blocks, list(range(i0, i0 + per_bank)), put_now)
 
-        def read_pages(first, count):
+        def read_pages(x_neg, wgt_neg, first, count):
             for i in range(PACK):
                 nc.vector.tensor_tensor(
                     x_neg[i][:, first : first + count],
@@ -170,11 +182,11 @@ def tile_list_glaze_firing_deviation_kernel(
                     ALU.mult,
                 )
 
-        def make_z(b, c):
+        def make_z(c, x_neg, clay_sb, z_banks, rounded):
             turned = []
             for block in range(CHUNK // P):
                 m0 = c * CHUNK + block * P
-                bank = take_bank()
+                bank = z_banks[(3 * c + block) % len(z_banks)]
                 for i in range(PACK):
                     nc.tensor.matmul(
                         bank[:, i * P : (i + 1) * P], lhsT=clay_sb[:, i * M + m0 : i * M + m0 + P], rhs=ident[:],
@@ -194,121 +206,132 @@ def tile_list_glaze_firing_deviation_kernel(
                     scale=-1.0,
                 )
                 turned.append(pairs)
-            bank = take_bank()
+            bank = z_banks[(3 * c + 2) % len(z_banks)]
             for block, pairs in enumerate(turned):
                 words = pairs[:].bitcast(F32)
                 for u in range(2):
                     at = (2 * block + u) * P
                     nc.tensor.transpose(bank[:, at : at + P], words[:, u * P : (u + 1) * P], ident[:])
             nc.scalar.copy(
-                z_rounded[c][:].bitcast(F32).rearrange("p (k m u) -> p k m u", k=CHUNK // P, u=2),
+                rounded.bitcast(F32).rearrange("p (k m u) -> p k m u", k=CHUNK // P, u=2),
                 bank[:].rearrange("p (k u m) -> p k m u", k=CHUNK // P, u=2),
             )
-            nc.vector.quantize_mx(out=z_codes[b][c][:].bitcast(FP8X4), scales=z_plane[b][c][:], in_=z_rounded[c][:])
 
-        def score_passes(c, passes):
-            for pair in range(N_TILES // 2):
-                bank = banks[3 * (c % 2) + pair]
-                for b in passes:
-                    for side in range(2):
-                        cols = slice((2 * pair + side) * P, (2 * pair + side + 1) * P)
-                        nc.tensor.matmul_mx(
-                            bank[:, side * CHUNK : (side + 1) * CHUNK],
-                            lhsT=wo_codes[b][:, cols].bitcast(FP8X4), lhsT_scale=wo_plane[b][:, cols],
-                            rhs=z_codes[b][c][:].bitcast(FP8X4), rhs_scale=z_plane[b][c][:],
-                            start=(b == 0 and side == 0), stop=(b == PASSES - 1 and side == 1),
-                        )
-
-        def finish(c):
-            view = out.rearrange("(t p) m -> p t m", p=P)
-            for pair in range(N_TILES // 2):
-                bank = banks[3 * (c % 2) + pair]
-                part = result[c][:, pair * BANK : (pair + 1) * BANK]
-                nc.vector.tensor_tensor(part, bank[:], part, ALU.subtract)
-                nc.sync.dma_start(
-                    view[:, 2 * pair : 2 * pair + 2, c * CHUNK : (c + 1) * CHUNK], part.rearrange("p (t m) -> p t m", t=2)
-                )
-
-        def load_target(c):
-            nc.sync.dma_start(
-                result[c].rearrange("p (t m) -> p t m", t=N_TILES),
-                target.rearrange("(t p) m -> p t m", p=P)[:, :, c * CHUNK : (c + 1) * CHUNK],
+        def quantize_z(b, first, count, rounded):
+            cols = slice(first, first + count)
+            nc.vector.quantize_mx(
+                out=z_codes[b][:, cols].bitcast(FP8X4),
+                scales=z_plane[b][:, cols],
+                in_=rounded,
             )
 
+        def score_passes(unit_no, passes):
+            half, t = divmod(unit_no, N_TILES)
+            bank = banks[unit_no % SCORE_BANKS]
+            rows = slice(t * P, (t + 1) * P)
+            cols = slice(half * BANK, (half + 1) * BANK)
+            for b in passes:
+                nc.tensor.matmul_mx(
+                    bank[:],
+                    lhsT=wo_codes[b][:, rows].bitcast(FP8X4), lhsT_scale=wo_plane[b][:, rows],
+                    rhs=z_codes[b][:, cols].bitcast(FP8X4), rhs_scale=z_plane[b][:, cols],
+                    start=(b == 0), stop=(b == PASSES - 1),
+                )
+
+        def finish(unit_no, result):
+            half, t = divmod(unit_no, N_TILES)
+            part = result[:, t * BANK : (t + 1) * BANK]
+            nc.vector.tensor_tensor(part, banks[unit_no % SCORE_BANKS][:], part, ALU.subtract)
+            nc.sync.dma_start(out[t * P : (t + 1) * P, half * BANK : (half + 1) * BANK], part)
+
+        def load_target(half, tag):
+            result = tile("result%d" % half, N_TILES * BANK, F32, tag=tag)
+            nc.sync.dma_start(
+                result[:].rearrange("p (t m) -> p t m", t=N_TILES),
+                target.rearrange("(t p) m -> p t m", p=P)[:, :, half * BANK : (half + 1) * BANK],
+            )
+            return result
+
         nc.vector.memset(table_scales[:].bitcast(I32), 0)
-        nc.vector.memset(wa_plane[:].bitcast(I32), 0)
-        nc.vector.memset(warm[:], 1.0)
+        nc.gpsimd.memset(warm[:], 1.0)
+        nc.gpsimd.memset(wa_plane[:].bitcast(I32), 0)
         nc.scalar.activation(warm[:, 0:1], warm[:, 1:2], ACT.Sqrt)
-        make_identity(nc, ident[:])
-        load_wb(0)
-        load_scale_rows(table_scales, tab_scales)
-        nc.sync.dma_start(table[:].bitcast(I32), tab_words[0].rearrange("p t i -> p (t i)").bitcast(I32))
-        nc.sync.dma_start(pick[:], offs)
-        nc.sync.dma_start(wa_codes[:].bitcast(I32), wa_words[0].bitcast(I32))
-        load_scale_rows(wa_plane, wa_scales)
-        nc.sync.dma_start(
+        load_scale_rows(nc.scalar, table_scales, tab_scales)
+        load_scale_rows(nc.gpsimd, wa_plane, wa_scales)
+        nc.gpsimd.dma_start(
             unit_cols[:].rearrange("p (b i) -> p b i", i=PACK), unit.rearrange("(b p i) -> p b i", p=P, i=PACK)
         )
-        nc.sync.dma_start(wgs_sb[:], wgs)
+        make_identity(nc, ident[:])
+        nc.sync.dma_start(pick[:], offs)
         nc.sync.dma_start(put[:], offs2)
         nc.sync.dma_start(read[:], offs3)
+        raw = load_wb(0)
+        nc.sync.dma_start(table[:].bitcast(I32), tab_words[0].rearrange("p t i -> p (t i)").bitcast(I32))
+        nc.sync.dma_start(wa_codes[:].bitcast(I32), wa_words[0].bitcast(I32))
+        nc.sync.dma_start(wgs_sb[:], wgs)
         for page in pages:
             nc.vector.memset(page[:], 0.0)
-        for piece in range(2):
-            quantize_wb(0, piece)
-        load_clay(0)
-        load_wb(1)
-        nc.sync.dma_start(wgt_neg[:], wgt)
-        load_wo(0)
         nc.vector.tensor_copy(v_scales[:], table_scales[:].indirect(pick[:]))
+        quantize_wb(0, raw, 256)
         for half in range(2):
             nc.vector.tensor_copy(v_words[half][:], table[:].indirect(pick[:, 32 * half : 32 * (half + 1)]))
+        raw = load_wb(1)
+        wgt_neg = tile("wgt_neg", M, F32, tag="scales_then_wgt")
+        nc.sync.dma_start(wgt_neg[:], wgt)
+        clay_sb = load_clay(0)
 
         low, high = [0, 1, 2, 3], [4, 5, 6, 7]
-        for blocks in ([0], [1], [2, 3]):
-            square_products(0, blocks)
-            roots(0, blocks)
-        square_products(0, high)
+        square_products(0, [0])
         for i in range(PACK):
-            root_and_put(0, high, [i])
-            if i < 2:
-                quantize_wb(1, i)
-        load_wb(2)
+            root_slices(0, [0], [i], True)
+        for blocks in ([1], [2, 3]):
+            square_products(0, blocks)
+            roots(0, blocks, True)
+        quantize_wb(1, raw, 512)
+        raw = load_wb(2)
+        square_products(0, high)
+        roots(0, high, True)
+        quantize_wb(2, raw, 512)
+        raw = load_wo(0)
         nc.scalar.mul(wgt_neg[:], wgt_neg[:], -1.0)
-        read_pages(0, M)
-        quantize_wo(0)
-        load_wo(1)
-        square_products(1, low)
-        roots(1, low)
-        square_products(1, high)
-        for piece in range(2):
-            quantize_wb(2, piece)
-        load_target(2)
+        read_pages(x_neg, wgt_neg, 0, M)
+        for blocks in (low, high):
+            square_products(1, blocks)
+            roots(1, blocks, False)
+        for i in range(PACK):
+            put_columns(1, i, 0, S)
+        quantize_wo(0, raw)
+        raw = load_wo(1)
         for c in range(CHUNKS):
-            make_z(0, c)
-        load_clay(1)
-        roots(1, high)
-        read_pages(0, M)
-        quantize_wo(1)
-        load_wo(2)
-        square_products(2, low)
-        roots(2, low)
-        square_products(2, high)
-        quantize_wo(2)
-        load_target(3)
+            make_z(c, x_neg, clay_sb, last_taken(PACK), z_rounded[c])
+        quantize_z(0, 0, M, z_whole[:])
+        clay_sb = load_clay(1)
+        quantize_wo(1, raw)
+        raw = load_wo(2)
+        read_pages(x_neg, wgt_neg, 0, M)
+        for blocks in (low, high):
+            square_products(2, blocks)
+            roots(2, blocks, False)
+        for i in range(PACK):
+            put_columns(2, i, 0, S)
+        results = [load_target(0, "squares_then_result")]
+        quantize_wo(2, raw)
+        results.append(load_target(1, "raw_then_result"))
         for c in range(CHUNKS):
-            make_z(1, c)
-        load_clay(2)
-        roots(2, high)
-        load_target(0)
-        load_target(1)
-        ring["order"] = [6, 7]
-        for c in range(2):
-            score_passes(c, [0, 1])
-        for c in range(CHUNKS):
-            read_pages(c * CHUNK, CHUNK)
-            make_z(2, c)
-            if c >= 2:
-                score_passes(c, [0, 1])
-            score_passes(c, [2])
-            finish(c)
+            make_z(c, x_neg, clay_sb, last_taken(PACK), z_rounded[c])
+        quantize_z(1, 0, M, z_whole[:])
+        clay_sb = load_clay(2)
+        for unit_no in range(SCORE_BANKS):
+            score_passes(unit_no, [0, 1])
+        x_last = tile("x_last", PACK * M, F32, tag="z_then_x")
+        x_neg = [x_last[:, i * M : (i + 1) * M] for i in range(PACK)]
+        for half in range(2):
+            z_half = tile("z_half%d" % half, PACK * BANK, BF16, tag="x_then_z%d" % half)
+            for k in range(2):
+                c = 2 * half + k
+                read_pages(x_neg, wgt_neg, c * CHUNK, CHUNK)
+                make_z(c, x_neg, clay_sb, banks[SCORE_BANKS:], z_half[:, k * PACK * CHUNK : (k + 1) * PACK * CHUNK])
+            quantize_z(2, half * BANK, BANK, z_half[:])
+        for unit_no in range(2 * N_TILES):
+            score_passes(unit_no, [2] if unit_no < SCORE_BANKS else [0, 1, 2])
+            finish(unit_no, results[unit_no // N_TILES])

@@ -43,10 +43,10 @@ def tile_list_glaze_firing_deviation_kernel(
         pick = tile("pick", S // 16, U16)
         put = tile("put", S // 16, U16)
         read = tile("read", M // 16, U16)
-        table = tile("table", T, U32, tag="table_then_clay")
-        table_scales = tile("table_scales", T, U8, tag="scales_then_wgt")
+        table = tile("table", T, U32, tag="staging")
+        table_scales = tile("table_scales", T, U8, tag="scales_then_clay")
         v_words = [tile("v_words%d" % half, BANK, U32) for half in range(2)]
-        v_scales = tile("v_scales", S, U8)
+        v_scales = [tile("v_scales%d" % half, BANK, U8) for half in range(2)]
         wa_codes = tile("wa_codes", 2 * H, U8)
         wa_plane = tile("wa_plane", H, U8)
         wb_codes = [tile("wb_codes%d" % b, R_PASS, U32) for b in range(PASSES)]
@@ -57,26 +57,25 @@ def tile_list_glaze_firing_deviation_kernel(
         wgs_sb = tile("wgs_sb", S, F32)
         pages = [tile("page%d" % i, T2, F32) for i in range(PACK)]
         squares = tile("squares", 8 * BANK, F32, tag="squares_then_result")
-        h_sb = [[tile("h%d_%d" % (side, i), S, F32) for i in range(PACK)] for side in range(2)]
+        h_sb = [[tile("h%d_%d" % (side, i), S, F32, tag="h%d_%d" % (side, i)) for i in range(PACK)] for side in range(2)]
         x_neg = [tile("x_neg%d" % i, M, F32, tag="x_then_z%d" % i)[:] for i in range(PACK)]
-        z_turned = [tile("z_turned%d" % k, R_PASS, BF16) for k in range(4)]
-        z_whole = tile("z_whole", PACK * M, BF16, tag="z_then_x")
-        z_rounded = [z_whole[:, c * PACK * CHUNK : (c + 1) * PACK * CHUNK] for c in range(CHUNKS)]
+        z_turned = [[tile("z_turned%d_%d" % (c, u), 2 * CHUNK, BF16) for u in range(2)] for c in range(CHUNKS)]
+        wgt_neg = tile("wgt_neg", M, F32)
         z_codes = [tile("z_codes%d" % b, M, U32) for b in range(PASSES)]
         z_plane = [tile("z_plane%d" % b, M, U8) for b in range(PASSES)]
         ident = tile("ident", P, F32)
         warm = tile("warm", 8, F32)
 
         banks = [ps.tile([P, BANK], F32, name="bank%d" % k) for k in range(8)]
-        ring = {"at": 0, "turned": 0}
+        ring = {"at": 0, "banks": banks}
 
         def take_bank():
-            bank = banks[ring["at"] % len(banks)]
+            bank = ring["banks"][ring["at"] % len(ring["banks"])]
             ring["at"] = ring["at"] + 1
             return bank
 
         def last_taken(count):
-            return [banks[(ring["at"] - count + k) % len(banks)] for k in range(count)]
+            return [ring["banks"][(ring["at"] - count + k) % len(ring["banks"])] for k in range(count)]
 
         def load_scale_rows(queue, plane, rows):
             for quadrant in range(4):
@@ -85,23 +84,33 @@ def tile_list_glaze_firing_deviation_kernel(
                     rows[0, 4 * quadrant : 4 * quadrant + 4, :].bitcast(I32),
                 )
 
-        def load_wb(b):
-            raw = tile("wb_raw%d" % b, PACK * R_PASS, F32, tag="raw_then_result")
-            nc.sync.dma_start(
+        def load_wb(b, queue, tag):
+            raw = tile("wb_raw%d" % b, PACK * R_PASS, F32, tag=tag)
+            queue.dma_start(
                 raw[:].rearrange("p (t c) -> p t c", t=PACK),
                 wb[:, b * R_PASS : (b + 1) * R_PASS].rearrange("(p t) c -> p t c", t=PACK),
             )
             return raw
 
         def load_wo(b):
-            raw = tile("wo_raw%d" % b, PACK * N, F32, tag="raw_then_result")
-            nc.sync.dma_start(raw[:], wo[b * R_PASS : (b + 1) * R_PASS, :].rearrange("(p t) n -> p (t n)", t=PACK))
+            raw = tile("wo_raw%d" % b, PACK * N, F32, tag="staging")
+            nc.scalar.dma_start(raw[:], wo[b * R_PASS : (b + 1) * R_PASS, :].rearrange("(p t) n -> p (t n)", t=PACK))
             return raw
 
         def load_clay(b):
-            clay_sb = tile("clay%d" % b, PACK * M, F32, tag="table_then_clay")
+            clay_sb = tile("clay%d" % b, PACK * M, F32, tag="scales_then_clay")
             nc.sync.dma_start(clay_sb[:], clay[b * R_PASS : (b + 1) * R_PASS, :].rearrange("(p t) m -> p (t m)", t=PACK))
-            return clay_sb
+            return [clay_sb[:, i * M : (i + 1) * M] for i in range(PACK)]
+
+        def load_last_clay():
+            b = PASSES - 1
+            rows = clay[b * R_PASS : (b + 1) * R_PASS, :].rearrange("(p t) m -> p t m", t=PACK)
+            slices = []
+            for i in range(PACK):
+                clay_sb = tile("clay_last%d" % i, M, F32, tag="h1_%d" % i)
+                nc.sync.dma_start(clay_sb[:], rows[:, i, :])
+                slices.append(clay_sb[:])
+            return slices
 
         def quantize_columns(name, raw, codes, plane, first, count):
             cols = slice(first, first + count)
@@ -123,7 +132,7 @@ def tile_list_glaze_firing_deviation_kernel(
         def square_products(b, blocks):
             for jb in blocks:
                 lhsT = v_words[jb // 4][:, (jb % 4) * P : (jb % 4 + 1) * P].bitcast(FP8X4)
-                lhsT_scale = v_scales[:, jb * P : (jb + 1) * P]
+                lhsT_scale = v_scales[jb // 4][:, (jb % 4) * P : (jb % 4 + 1) * P]
                 operands = (
                     (wa_codes[:, 2 * b * R_PASS : 2 * (b + 1) * R_PASS].bitcast(FP4X4), wa_plane[:, b * R_PASS : (b + 1) * R_PASS]),
                     (wb_codes[b][:].bitcast(FP8X4), wb_plane[b][:]),
@@ -138,17 +147,14 @@ def tile_list_glaze_firing_deviation_kernel(
                         ACT.Square,
                     )
 
-        def put_columns(b, i, first, count):
+        def put_columns(i, first, h):
+            count = h.shape[1]
             nc.vector.tensor_tensor(
-                pages[i][:].indirect(put[:, first // 16 : (first + count) // 16]),
-                h_sb[b % 2][i][:, first : first + count],
-                wgs_sb[:, first : first + count],
-                ALU.mult,
+                pages[i][:].indirect(put[:, first // 16 : (first + count) // 16]), h, wgs_sb[:, first : first + count], ALU.mult
             )
 
-        def root_slices(b, blocks, slices, put_now):
+        def add_squares(blocks, slices):
             count = len(blocks) * P
-            first = blocks[0] * P
             bank = take_bank()
             for place, i in enumerate(slices):
                 for step, jb in enumerate(blocks):
@@ -159,59 +165,58 @@ def tile_list_glaze_firing_deviation_kernel(
                             bank[:, at : at + P], lhsT=squares[:, src : src + P], rhs=ident[:],
                             is_transpose=True, start=(which == 0), stop=(which == 1),
                         )
-            for place, i in enumerate(slices):
-                h = h_sb[b % 2][i][:, first : first + count]
-                nc.scalar.activation(
-                    h, bank[:, place * count : (place + 1) * count], ACT.Sqrt,
-                    bias=unit_cols[:, b * PACK + i : b * PACK + i + 1],
-                )
-                if put_now:
-                    put_columns(b, i, first, count)
+            return bank
 
-        def roots(b, blocks, put_now):
-            per_bank = BANK // (len(blocks) * P)
-            for i0 in range(0, PACK, per_bank):
-                root_slices(b, blocks, list(range(i0, i0 + per_bank)), put_now)
+        def root(b, i, h, sums):
+            nc.scalar.activation(h, sums, ACT.Sqrt, bias=unit_cols[:, b * PACK + i : b * PACK + i + 1])
 
-        def read_pages(x_neg, wgt_neg, first, count):
-            for i in range(PACK):
-                nc.vector.tensor_tensor(
-                    x_neg[i][:, first : first + count],
-                    pages[i][:].indirect(read[:, first // 16 : (first + count) // 16]),
-                    wgt_neg[:, first : first + count],
-                    ALU.mult,
-                )
+        def roots(b, blocks, slices, per_bank, put_now):
+            count = len(blocks) * P
+            first = blocks[0] * P
+            for at in range(0, len(slices), per_bank):
+                group = slices[at : at + per_bank]
+                bank = add_squares(blocks, group)
+                for place, i in enumerate(group):
+                    h = h_sb[b % 2][i][:, first : first + count]
+                    root(b, i, h, bank[:, place * count : (place + 1) * count])
+                    if put_now:
+                        put_columns(i, first, h)
 
-        def make_z(c, x_neg, clay_sb, z_banks, rounded):
-            turned = []
-            for block in range(CHUNK // P):
-                m0 = c * CHUNK + block * P
-                bank = z_banks[(3 * c + block) % len(z_banks)]
-                for i in range(PACK):
+        def read_page(i, first, x):
+            count = x.shape[1]
+            nc.vector.tensor_tensor(
+                x, pages[i][:].indirect(read[:, first // 16 : (first + count) // 16]), wgt_neg[:, first : first + count], ALU.mult
+            )
+
+        def turn_pair(c, u, x_pair, clay_sb, bank):
+            for k in range(CHUNK // P):
+                for e in range(2):
+                    at = (2 * k + e) * P
+                    m0 = c * CHUNK + k * P
                     nc.tensor.matmul(
-                        bank[:, i * P : (i + 1) * P], lhsT=clay_sb[:, i * M + m0 : i * M + m0 + P], rhs=ident[:],
-                        is_transpose=True, start=(i == 0), stop=False,
+                        bank[:, at : at + P], lhsT=clay_sb[2 * u + e][:, m0 : m0 + P], rhs=ident[:],
+                        is_transpose=True, start=(k == 0 and e == 0), stop=False,
                     )
-                for i in range(PACK):
+            for e in range(2):
+                for k in range(CHUNK // P):
+                    at = (2 * k + e) * P
                     nc.tensor.matmul(
-                        bank[:, i * P : (i + 1) * P], lhsT=x_neg[i][:, m0 : m0 + P], rhs=ident[:],
-                        is_transpose=True, start=False, stop=(i == PACK - 1),
+                        bank[:, at : at + P], lhsT=x_pair[e][:, k * P : (k + 1) * P], rhs=ident[:],
+                        is_transpose=True, start=False, stop=(k == CHUNK // P - 1 and e == 1),
                     )
-                pairs = z_turned[ring["turned"] % len(z_turned)]
-                ring["turned"] = ring["turned"] + 1
-                nc.scalar.activation(
-                    pairs[:].rearrange("m (u p e) -> m u p e", u=2, e=2),
-                    bank[:].rearrange("m (u e p) -> m u p e", u=2, e=2),
-                    ACT.Copy,
-                    scale=-1.0,
-                )
-                turned.append(pairs)
-            bank = z_banks[(3 * c + 2) % len(z_banks)]
-            for block, pairs in enumerate(turned):
-                words = pairs[:].bitcast(F32)
-                for u in range(2):
-                    at = (2 * block + u) * P
-                    nc.tensor.transpose(bank[:, at : at + P], words[:, u * P : (u + 1) * P], ident[:])
+            nc.scalar.activation(
+                z_turned[c][u][:].rearrange("m (k p e) -> m k p e", k=CHUNK // P, e=2),
+                bank[:].rearrange("m (k e p) -> m k p e", k=CHUNK // P, e=2),
+                ACT.Copy,
+                scale=-1.0,
+            )
+
+        def turn_back(c, bank, rounded):
+            for u in range(2):
+                words = z_turned[c][u][:].bitcast(F32)
+                for k in range(CHUNK // P):
+                    at = (2 * k + u) * P
+                    nc.tensor.transpose(bank[:, at : at + P], words[:, k * P : (k + 1) * P], ident[:])
             nc.scalar.copy(
                 rounded.bitcast(F32).rearrange("p (k m u) -> p k m u", k=CHUNK // P, u=2),
                 bank[:].rearrange("p (k u m) -> p k m u", k=CHUNK // P, u=2),
@@ -225,9 +230,9 @@ def tile_list_glaze_firing_deviation_kernel(
                 in_=rounded,
             )
 
-        def score_passes(unit_no, passes):
+        def score_passes(score_banks, unit_no, passes):
             half, t = divmod(unit_no, N_TILES)
-            bank = banks[unit_no % SCORE_BANKS]
+            bank = score_banks[unit_no % SCORE_BANKS]
             rows = slice(t * P, (t + 1) * P)
             cols = slice(half * BANK, (half + 1) * BANK)
             for b in passes:
@@ -238,10 +243,10 @@ def tile_list_glaze_firing_deviation_kernel(
                     start=(b == 0), stop=(b == PASSES - 1),
                 )
 
-        def finish(unit_no, result):
+        def finish(score_banks, unit_no, result):
             half, t = divmod(unit_no, N_TILES)
             part = result[:, t * BANK : (t + 1) * BANK]
-            nc.vector.tensor_tensor(part, banks[unit_no % SCORE_BANKS][:], part, ALU.subtract)
+            nc.vector.tensor_tensor(part, score_banks[unit_no % SCORE_BANKS][:], part, ALU.subtract)
             nc.sync.dma_start(out[t * P : (t + 1) * P, half * BANK : (half + 1) * BANK], part)
 
         def load_target(half, tag):
@@ -253,85 +258,118 @@ def tile_list_glaze_firing_deviation_kernel(
             return result
 
         nc.vector.memset(table_scales[:].bitcast(I32), 0)
-        nc.gpsimd.memset(warm[:], 1.0)
+        make_identity(nc, ident[:])
         nc.gpsimd.memset(wa_plane[:].bitcast(I32), 0)
-        nc.scalar.activation(warm[:, 0:1], warm[:, 1:2], ACT.Sqrt)
+        nc.vector.memset(warm[:], 1.0)
         load_scale_rows(nc.scalar, table_scales, tab_scales)
+        nc.scalar.activation(warm[:, 0:1], warm[:, 1:2], ACT.Sqrt)
         load_scale_rows(nc.gpsimd, wa_plane, wa_scales)
         nc.gpsimd.dma_start(
             unit_cols[:].rearrange("p (b i) -> p b i", i=PACK), unit.rearrange("(b p i) -> p b i", p=P, i=PACK)
         )
-        make_identity(nc, ident[:])
         nc.sync.dma_start(pick[:], offs)
         nc.sync.dma_start(put[:], offs2)
         nc.sync.dma_start(read[:], offs3)
-        raw = load_wb(0)
+        raw = load_wb(0, nc.sync, "z_then_x")
         nc.sync.dma_start(table[:].bitcast(I32), tab_words[0].rearrange("p t i -> p (t i)").bitcast(I32))
         nc.sync.dma_start(wa_codes[:].bitcast(I32), wa_words[0].bitcast(I32))
         nc.sync.dma_start(wgs_sb[:], wgs)
         for page in pages:
             nc.vector.memset(page[:], 0.0)
-        nc.vector.tensor_copy(v_scales[:], table_scales[:].indirect(pick[:]))
         quantize_wb(0, raw, 256)
         for half in range(2):
+            nc.vector.tensor_copy(v_scales[half][:], table_scales[:].indirect(pick[:, 32 * half : 32 * (half + 1)]))
             nc.vector.tensor_copy(v_words[half][:], table[:].indirect(pick[:, 32 * half : 32 * (half + 1)]))
-        raw = load_wb(1)
-        wgt_neg = tile("wgt_neg", M, F32, tag="scales_then_wgt")
-        nc.sync.dma_start(wgt_neg[:], wgt)
+        raw = load_wb(1, nc.sync, "staging")
         clay_sb = load_clay(0)
+        z_whole = tile("z_whole", PACK * M, BF16, tag="z_then_x")
+        z_rounded = [z_whole[:, c * PACK * CHUNK : (c + 1) * PACK * CHUNK] for c in range(CHUNKS)]
 
         low, high = [0, 1, 2, 3], [4, 5, 6, 7]
-        square_products(0, [0])
-        for i in range(PACK):
-            root_slices(0, [0], [i], True)
-        for blocks in ([1], [2, 3]):
+        every = list(range(PACK))
+
+        def z_pass(b, clay_sb, z_banks):
+            for c in range(CHUNKS):
+                for u in range(2):
+                    x_pair = [x[:, c * CHUNK : (c + 1) * CHUNK] for x in x_neg[2 * u : 2 * u + 2]]
+                    turn_pair(c, u, x_pair, clay_sb, z_banks[(3 * c + u) % len(z_banks)])
+                turn_back(c, z_banks[(3 * c + 2) % len(z_banks)], z_rounded[c])
+            quantize_z(b, 0, M, z_whole[:])
+
+        for step, blocks in enumerate(([0], [1], [2], [3], [4, 5], [6, 7])):
             square_products(0, blocks)
-            roots(0, blocks, True)
-        quantize_wb(1, raw, 512)
-        raw = load_wb(2)
-        square_products(0, high)
-        roots(0, high, True)
+            roots(0, blocks, every, 1 if step == 0 else PACK // len(blocks), True)
+            if step == 3:
+                quantize_wb(1, raw, 512)
+                wgt_raw = tile("wgt_raw", M, F32, tag="staging")
+                nc.scalar.dma_start(wgt_raw[:], wgt)
+        nc.scalar.mul(wgt_neg[:], wgt_raw[:], -1.0)
+        raw = load_wb(2, nc.scalar, "staging")
+        for i in every:
+            read_page(i, 0, x_neg[i])
+        square_products(1, low)
+        roots(1, low, every, 1, True)
         quantize_wb(2, raw, 512)
         raw = load_wo(0)
-        nc.scalar.mul(wgt_neg[:], wgt_neg[:], -1.0)
-        read_pages(x_neg, wgt_neg, 0, M)
-        for blocks in (low, high):
-            square_products(1, blocks)
-            roots(1, blocks, False)
-        for i in range(PACK):
-            put_columns(1, i, 0, S)
+        square_products(1, high)
+        roots(1, high, every, 1, True)
         quantize_wo(0, raw)
         raw = load_wo(1)
-        for c in range(CHUNKS):
-            make_z(c, x_neg, clay_sb, last_taken(PACK), z_rounded[c])
-        quantize_z(0, 0, M, z_whole[:])
+        z_pass(0, clay_sb, last_taken(PACK))
         clay_sb = load_clay(1)
+        for i in every:
+            read_page(i, 0, x_neg[i])
+        last = PACK - 1
+        square_products(2, low)
+        roots(2, low, every[:last], 1, True)
+        held = [add_squares(low, [last])]
+        free = [bank for bank in banks if bank is not held[0]]
+        ring["banks"] = free
         quantize_wo(1, raw)
         raw = load_wo(2)
-        read_pages(x_neg, wgt_neg, 0, M)
-        for blocks in (low, high):
-            square_products(2, blocks)
-            roots(2, blocks, False)
-        for i in range(PACK):
-            put_columns(2, i, 0, S)
-        results = [load_target(0, "squares_then_result")]
+        square_products(2, high)
+        roots(2, high, every[:last], 1, True)
+        z_banks = last_taken(PACK)
+        z_banks = z_banks[1:] + z_banks[:1]
+        held.append(add_squares(high, [last]))
         quantize_wo(2, raw)
-        results.append(load_target(1, "raw_then_result"))
-        for c in range(CHUNKS):
-            make_z(c, x_neg, clay_sb, last_taken(PACK), z_rounded[c])
-        quantize_z(1, 0, M, z_whole[:])
-        clay_sb = load_clay(2)
+        results = [load_target(0, "squares_then_result"), load_target(1, "staging")]
+        last_clay = load_last_clay()
+        z_pass(1, clay_sb, z_banks)
+        others = [bank for bank in free if bank is not held[1]]
+        score_banks = others[:SCORE_BANKS]
+        z_banks = held + others[SCORE_BANKS:]
+        x_last = tile("x_last", PACK * M + S, F32, tag="z_then_x")
+        x_neg = [x_last[:, i * M : (i + 1) * M] for i in every]
+        h_last = x_last[:, PACK * M :]
+        for i in range(2):
+            read_page(i, 0, x_neg[i])
+        for half in range(2):
+            root(PASSES - 1, last, h_last[:, half * BANK : (half + 1) * BANK], held[half][:])
+        put_columns(last, 0, h_last)
         for unit_no in range(SCORE_BANKS):
-            score_passes(unit_no, [0, 1])
-        x_last = tile("x_last", PACK * M, F32, tag="z_then_x")
-        x_neg = [x_last[:, i * M : (i + 1) * M] for i in range(PACK)]
+            score_passes(score_banks, unit_no, [0, 1])
+        ring["banks"] = z_banks
+        ring["at"] = 0
+
+        def pair(c, u):
+            return [x[:, c * CHUNK : (c + 1) * CHUNK] for x in x_neg[2 * u : 2 * u + 2]]
+
+        for c in range(CHUNKS):
+            turn_pair(c, 0, pair(c, 0), last_clay, take_bank())
         for half in range(2):
             z_half = tile("z_half%d" % half, PACK * BANK, BF16, tag="x_then_z%d" % half)
+            for c in range(2 * half, 2 * half + 2):
+                for e in range(2):
+                    read_page(2 + e, c * CHUNK, pair(c, 1)[e])
+                turn_pair(c, 1, pair(c, 1), last_clay, take_bank())
             for k in range(2):
-                c = 2 * half + k
-                read_pages(x_neg, wgt_neg, c * CHUNK, CHUNK)
-                make_z(c, x_neg, clay_sb, banks[SCORE_BANKS:], z_half[:, k * PACK * CHUNK : (k + 1) * PACK * CHUNK])
+                turn_back(2 * half + k, take_bank(), z_half[:, k * PACK * CHUNK : (k + 1) * PACK * CHUNK])
             quantize_z(2, half * BANK, BANK, z_half[:])
+            if half == 1:
+                for unit_no in range(SCORE_BANKS):
+                    score_passes(score_banks, unit_no, [2])
         for unit_no in range(2 * N_TILES):
-            score_passes(unit_no, [2] if unit_no < SCORE_BANKS else [0, 1, 2])
-            finish(unit_no, results[unit_no // N_TILES])
+            if unit_no >= SCORE_BANKS:
+                score_passes(score_banks, unit_no, [0, 1, 2])
+            finish(score_banks, unit_no, results[unit_no // N_TILES])

@@ -27,6 +27,7 @@ CHUNKS = M // CHUNK
 PIECE = 256
 N_TILES = N // P
 SCORE_BANKS = 5
+ROUNDED_BUFS = 5
 
 
 def tile_list_glaze_firing_deviation_kernel(
@@ -43,18 +44,14 @@ def tile_list_glaze_firing_deviation_kernel(
         pick = tile("pick", S // 16, U16)
         put = tile("put", S // 16, U16)
         read = tile("read", M // 16, U16)
-        table = tile("table", T, U32, tag="staging")
-        table_scales = tile("table_scales", T, U8, tag="scales_then_clay")
+        table_scales = tile("table_scales", T, U8, tag="scales_then_wgs")
         v_words = [tile("v_words%d" % half, BANK, U32) for half in range(2)]
         v_scales = [tile("v_scales%d" % half, BANK, U8) for half in range(2)]
-        wa_codes = tile("wa_codes", 2 * H, U8)
         wa_plane = tile("wa_plane", H, U8)
         wb_codes = [tile("wb_codes%d" % b, R_PASS, U32) for b in range(PASSES)]
         wb_plane = [tile("wb_plane%d" % b, R_PASS, U8) for b in range(PASSES)]
         wo_codes = [tile("wo_codes%d" % b, N, U32) for b in range(PASSES)]
         wo_plane = [tile("wo_plane%d" % b, N, U8) for b in range(PASSES)]
-        unit_cols = tile("unit_cols", PASSES * PACK, F32)
-        wgs_sb = tile("wgs_sb", S, F32)
         pages = [tile("page%d" % i, T2, F32) for i in range(PACK)]
         squares = tile("squares", 8 * BANK, F32, tag="squares_then_result")
         h_sb = [[tile("h%d_%d" % (side, i), S, F32, tag="h%d_%d" % (side, i)) for i in range(PACK)] for side in range(2)]
@@ -64,7 +61,6 @@ def tile_list_glaze_firing_deviation_kernel(
         z_codes = [tile("z_codes%d" % b, M, U32) for b in range(PASSES)]
         z_plane = [tile("z_plane%d" % b, M, U8) for b in range(PASSES)]
         ident = tile("ident", P, F32)
-        warm = tile("warm", 8, F32)
 
         banks = [ps.tile([P, BANK], F32, name="bank%d" % k) for k in range(8)]
         ring = {"at": 0, "banks": banks}
@@ -98,7 +94,7 @@ def tile_list_glaze_firing_deviation_kernel(
             return raw
 
         def load_clay(b):
-            clay_sb = tile("clay%d" % b, PACK * M, F32, tag="scales_then_clay")
+            clay_sb = tile("clay%d" % b, PACK * M, F32, tag="rounded_then_clay")
             nc.sync.dma_start(clay_sb[:], clay[b * R_PASS : (b + 1) * R_PASS, :].rearrange("(p t) m -> p (t m)", t=PACK))
             return [clay_sb[:, i * M : (i + 1) * M] for i in range(PACK)]
 
@@ -112,9 +108,9 @@ def tile_list_glaze_firing_deviation_kernel(
                 slices.append(clay_sb[:])
             return slices
 
-        def quantize_columns(name, raw, codes, plane, first, count):
+        def quantize_columns(name, raw, codes, plane, first, count, tag="rounded", bufs=ROUNDED_BUFS):
             cols = slice(first, first + count)
-            rounded = tile("%s_rounded%d" % (name, first), PACK * count, BF16, tag="rounded", bufs=6)
+            rounded = tile("%s_rounded%d" % (name, first), PACK * count, BF16, tag=tag, bufs=bufs)
             nc.scalar.copy(
                 rounded[:].rearrange("p (c e t) -> p c t e", e=4, t=PACK),
                 raw[:].rearrange("p (t c) -> p t c", t=PACK)[:, :, cols].rearrange("p t (c e) -> p c t e", e=4),
@@ -257,31 +253,38 @@ def tile_list_glaze_firing_deviation_kernel(
             )
             return result
 
-        nc.vector.memset(table_scales[:].bitcast(I32), 0)
+        warm_in = tile("warm_in", 8, F32, tag="staging")
+        warm_out = tile("warm_out", 8, F32, tag="warm_then_wa")
+        nc.gpsimd.memset(warm_in[:], 1.0)
+        nc.gpsimd.memset(table_scales[:].bitcast(I32), 0)
         make_identity(nc, ident[:])
-        nc.gpsimd.memset(wa_plane[:].bitcast(I32), 0)
-        nc.vector.memset(warm[:], 1.0)
-        load_scale_rows(nc.scalar, table_scales, tab_scales)
-        nc.scalar.activation(warm[:, 0:1], warm[:, 1:2], ACT.Sqrt)
-        load_scale_rows(nc.gpsimd, wa_plane, wa_scales)
-        nc.gpsimd.dma_start(
-            unit_cols[:].rearrange("p (b i) -> p b i", i=PACK), unit.rearrange("(b p i) -> p b i", p=P, i=PACK)
-        )
+        nc.scalar.activation(warm_out[:, 0:1], warm_in[:, 0:1], ACT.Sqrt)
         nc.sync.dma_start(pick[:], offs)
+        raw = load_wb(0, nc.sync, "z_then_x")
         nc.sync.dma_start(put[:], offs2)
         nc.sync.dma_start(read[:], offs3)
-        raw = load_wb(0, nc.sync, "z_then_x")
+        load_scale_rows(nc.sync, table_scales, tab_scales)
+        table = tile("table", T, U32, tag="staging")
         nc.sync.dma_start(table[:].bitcast(I32), tab_words[0].rearrange("p t i -> p (t i)").bitcast(I32))
+        wa_codes = tile("wa_codes", 2 * H, U8, tag="warm_then_wa")
         nc.sync.dma_start(wa_codes[:].bitcast(I32), wa_words[0].bitcast(I32))
-        nc.sync.dma_start(wgs_sb[:], wgs)
-        for page in pages:
+        for page in pages[:-1]:
             nc.vector.memset(page[:], 0.0)
-        quantize_wb(0, raw, 256)
+        nc.vector.memset(wa_plane[:].bitcast(I32), 0)
+        load_scale_rows(nc.sync, wa_plane, wa_scales)
+        nc.vector.memset(pages[-1][:], 0.0)
+        quantize_columns("wb0", raw, wb_codes[0], wb_plane[0], 0, PIECE, "rounded_then_unit", 1)
+        quantize_columns("wb0", raw, wb_codes[0], wb_plane[0], PIECE, PIECE)
+        unit_cols = tile("unit_cols", PASSES * PACK, F32, tag="rounded_then_unit")
+        nc.sync.dma_start(
+            unit_cols[:].rearrange("p (b i) -> p b i", i=PACK), unit.rearrange("(b p i) -> p b i", p=P, i=PACK)
+        )
         for half in range(2):
             nc.vector.tensor_copy(v_scales[half][:], table_scales[:].indirect(pick[:, 32 * half : 32 * (half + 1)]))
             nc.vector.tensor_copy(v_words[half][:], table[:].indirect(pick[:, 32 * half : 32 * (half + 1)]))
+        wgs_sb = tile("wgs_sb", S, F32, tag="scales_then_wgs")
+        nc.sync.dma_start(wgs_sb[:], wgs)
         raw = load_wb(1, nc.sync, "staging")
-        clay_sb = load_clay(0)
         z_whole = tile("z_whole", PACK * M, BF16, tag="z_then_x")
         z_rounded = [z_whole[:, c * PACK * CHUNK : (c + 1) * PACK * CHUNK] for c in range(CHUNKS)]
 
@@ -300,17 +303,20 @@ def tile_list_glaze_firing_deviation_kernel(
             square_products(0, blocks)
             roots(0, blocks, every, 1 if step == 0 else PACK // len(blocks), True)
             if step == 3:
-                quantize_wb(1, raw, 512)
+                quantize_columns("wb1", raw, wb_codes[1], wb_plane[1], 0, PIECE)
+                quantize_columns("wb1", raw, wb_codes[1], wb_plane[1], PIECE, PIECE, "rounded_then_clay", 1)
+                clay_sb = load_clay(0)
+                raw = load_wb(2, nc.scalar, "staging")
+            if step == 4:
+                quantize_wb(2, raw, PIECE)
                 wgt_raw = tile("wgt_raw", M, F32, tag="staging")
                 nc.scalar.dma_start(wgt_raw[:], wgt)
         nc.scalar.mul(wgt_neg[:], wgt_raw[:], -1.0)
-        raw = load_wb(2, nc.scalar, "staging")
+        raw = load_wo(0)
         for i in every:
             read_page(i, 0, x_neg[i])
         square_products(1, low)
         roots(1, low, every, 1, True)
-        quantize_wb(2, raw, 512)
-        raw = load_wo(0)
         square_products(1, high)
         roots(1, high, every, 1, True)
         quantize_wo(0, raw)

from contextlib import ExitStack

import concourse.mybir as mybir
from concourse.masks import make_identity

K, T, S, M, T2, H, N = 512, 4096, 1024, 1024, 2048, 1536, 768
FLOPS = 2 * (2 * K * H * S + H * N * M)

F32 = mybir.dt.float32
BF16 = mybir.dt.bfloat16
I32 = mybir.dt.int32
U32 = mybir.dt.uint32
U16 = mybir.dt.uint16
U8 = mybir.dt.uint8
FP8X4 = mybir.dt.float8_e4m3fn_x4
FP4X4 = mybir.dt.float4_e2m1fn_x4
ACT = mybir.ActivationFunctionType
ALU = mybir.AluOpType

P = 128
PACK = 4
R_PASS = P * PACK
PASSES = H // R_PASS
BANK = 512
CHUNK = 256
CHUNKS = M // CHUNK
PIECE = 256
N_TILES = N // P
SCORE_BANKS = 5
ROUNDED_BUFS = 5


def tile_list_glaze_firing_deviation_kernel(
    tc, tab_words, tab_scales, offs, offs2, offs3, wa_words, wa_scales, wb, unit, wgs, wgt, clay, wo, target, out
):
    nc = tc.nc
    with ExitStack() as ctx:
        sb = ctx.enter_context(tc.tile_pool(name="sb", bufs=1))
        ps = ctx.enter_context(tc.psum_pool(name="ps", bufs=1))

        def tile(name, cols, dtype, tag="", bufs=None):
            return sb.tile([P, cols], dtype, name=name, tag=tag or name, bufs=bufs, align_bytes=64)

        pick = tile("pick", S // 16, U16)
        put = tile("put", S // 16, U16)
        read = tile("read", M // 16, U16)
        table_scales = tile("table_scales", T, U8, tag="scales_then_wgs")
        v_words = [tile("v_words%d" % half, BANK, U32) for half in range(2)]
        v_scales = [tile("v_scales%d" % half, BANK, U8) for half in range(2)]
        wa_plane = tile("wa_plane", H, U8)
        wb_codes = [tile("wb_codes%d" % b, R_PASS, U32) for b in range(PASSES)]
        wb_plane = [tile("wb_plane%d" % b, R_PASS, U8) for b in range(PASSES)]
        wo_codes = [tile("wo_codes%d" % b, N, U32) for b in range(PASSES)]
        wo_plane = [tile("wo_plane%d" % b, N, U8) for b in range(PASSES)]
        pages = [tile("page%d" % i, T2, F32) for i in range(PACK)]
        squares = tile("squares", 8 * BANK, F32, tag="squares_then_result")
        h_sb = [[tile("h%d_%d" % (side, i), S, F32, tag="h%d_%d" % (side, i)) for i in range(PACK)] for side in range(2)]
        x_neg = [tile("x_neg%d" % i, M, F32, tag="x_then_z%d" % i)[:] for i in range(PACK)]
        z_turned = [[tile("z_turned%d_%d" % (c, u), 2 * CHUNK, BF16) for u in range(2)] for c in range(CHUNKS)]
        wgt_neg = tile("wgt_neg", M, F32)
        z_codes = [tile("z_codes%d" % b, M, U32) for b in range(PASSES)]
        z_plane = [tile("z_plane%d" % b, M, U8) for b in range(PASSES)]
        ident = tile("ident", P, F32)

        banks = [ps.tile([P, BANK], F32, name="bank%d" % k) for k in range(8)]
        ring = {"at": 0, "banks": banks}

        def take_bank():
            bank = ring["banks"][ring["at"] % len(ring["banks"])]
            ring["at"] = ring["at"] + 1
            return bank

        def last_taken(count):
            return [ring["banks"][(ring["at"] - count + k) % len(ring["banks"])] for k in range(count)]

        def load_scale_rows(queue, plane, rows):
            for quadrant in range(4):
                queue.dma_start(
                    plane[32 * quadrant : 32 * quadrant + 4, :].bitcast(I32),
                    rows[0, 4 * quadrant : 4 * quadrant + 4, :].bitcast(I32),
                )

        def load_wb(b, queue, tag):
            raw = tile("wb_raw%d" % b, PACK * R_PASS, F32, tag=tag)
            queue.dma_start(
                raw[:].rearrange("p (t c) -> p t c", t=PACK),
                wb[:, b * R_PASS : (b + 1) * R_PASS].rearrange("(p t) c -> p t c", t=PACK),
            )
            return raw

        def load_wo(b):
            raw = tile("wo_raw%d" % b, PACK * N, F32, tag="staging")
            nc.scalar.dma_start(raw[:], wo[b * R_PASS : (b + 1) * R_PASS, :].rearrange("(p t) n -> p (t n)", t=PACK))
            return raw

        def load_clay(b):
            clay_sb = tile("clay%d" % b, PACK * M, F32, tag="rounded_then_clay")
            nc.sync.dma_start(clay_sb[:], clay[b * R_PASS : (b + 1) * R_PASS, :].rearrange("(p t) m -> p (t m)", t=PACK))
            return [clay_sb[:, i * M : (i + 1) * M] for i in range(PACK)]

        def load_last_clay():
            b = PASSES - 1
            rows = clay[b * R_PASS : (b + 1) * R_PASS, :].rearrange("(p t) m -> p t m", t=PACK)
            slices = []
            for i in range(PACK):
                clay_sb = tile("clay_last%d" % i, M, F32, tag="h1_%d" % i)
                nc.sync.dma_start(clay_sb[:], rows[:, i, :])
                slices.append(clay_sb[:])
            return slices

        def quantize_columns(name, raw, codes, plane, first, count, tag="rounded", bufs=ROUNDED_BUFS):
            cols = slice(first, first + count)
            rounded = tile("%s_rounded%d" % (name, first), PACK * count, BF16, tag=tag, bufs=bufs)
            nc.scalar.copy(
                rounded[:].rearrange("p (c e t) -> p c t e", e=4, t=PACK),
                raw[:].rearrange("p (t c) -> p t c", t=PACK)[:, :, cols].rearrange("p t (c e) -> p c t e", e=4),
            )
            nc.vector.quantize_mx(out=codes[:, cols].bitcast(FP8X4), scales=plane[:, cols], in_=rounded[:])

        def quantize_wb(b, raw, width):
            for first in range(0, R_PASS, width):
                quantize_columns("wb%d" % b, raw, wb_codes[b], wb_plane[b], first, width)

        def quantize_wo(b, raw):
            quantize_columns("wo%d" % b, raw, wo_codes[b], wo_plane[b], 0, 512)
            quantize_columns("wo%d" % b, raw, wo_codes[b], wo_plane[b], 512, 256)

        def square_products(b, blocks):
            for jb in blocks:
                lhsT = v_words[jb // 4][:, (jb % 4) * P : (jb % 4 + 1) * P].bitcast(FP8X4)
                lhsT_scale = v_scales[jb // 4][:, (jb % 4) * P : (jb % 4 + 1) * P]
                operands = (
                    (wa_codes[:, 2 * b * R_PASS : 2 * (b + 1) * R_PASS].bitcast(FP4X4), wa_plane[:, b * R_PASS : (b + 1) * R_PASS]),
                    (wb_codes[b][:].bitcast(FP8X4), wb_plane[b][:]),
                )
                for which, (rhs, rhs_scale) in enumerate(operands):
                    bank = take_bank()
                    nc.tensor.matmul_mx(bank[:], lhsT=lhsT, lhsT_scale=lhsT_scale, rhs=rhs, rhs_scale=rhs_scale, start=True, stop=True)
                    at = (2 * (jb % 4) + which) * BANK
                    nc.scalar.activation(
                        squares[:, at : at + BANK].rearrange("p (i q) -> p i q", i=PACK),
                        bank[:].rearrange("p (q i) -> p i q", i=PACK),
                        ACT.Square,
                    )

        def put_columns(i, first, h):
            count = h.shape[1]
            nc.vector.tensor_tensor(
                pages[i][:].indirect(put[:, first // 16 : (first + count) // 16]), h, wgs_sb[:, first : first + count], ALU.mult
            )

        def add_squares(blocks, slices):
            count = len(blocks) * P
            bank = take_bank()
            for place, i in enumerate(slices):
                for step, jb in enumerate(blocks):
                    at = place * count + step * P
                    for which in range(2):
                        src = (2 * (jb % 4) + which) * BANK + i * P
                        nc.tensor.matmul(
                            bank[:, at : at + P], lhsT=squares[:, src : src + P], rhs=ident[:],
                            is_transpose=True, start=(which == 0), stop=(which == 1),
                        )
            return bank

        def root(b, i, h, sums):
            nc.scalar.activation(h, sums, ACT.Sqrt, bias=unit_cols[:, b * PACK + i : b * PACK + i + 1])

        def roots(b, blocks, slices, per_bank, put_now):
            count = len(blocks) * P
            first = blocks[0] * P
            for at in range(0, len(slices), per_bank):
                group = slices[at : at + per_bank]
                bank = add_squares(blocks, group)
                for place, i in enumerate(group):
                    h = h_sb[b % 2][i][:, first : first + count]
                    root(b, i, h, bank[:, place * count : (place + 1) * count])
                    if put_now:
                        put_columns(i, first, h)

        def read_page(i, first, x):
            count = x.shape[1]
            nc.vector.tensor_tensor(
                x, pages[i][:].indirect(read[:, first // 16 : (first + count) // 16]), wgt_neg[:, first : first + count], ALU.mult
            )

        def turn_pair(c, u, x_pair, clay_sb, bank):
            for k in range(CHUNK // P):
                for e in range(2):
                    at = (2 * k + e) * P
                    m0 = c * CHUNK + k * P
                    nc.tensor.matmul(
                        bank[:, at : at + P], lhsT=clay_sb[2 * u + e][:, m0 : m0 + P], rhs=ident[:],
                        is_transpose=True, start=(k == 0 and e == 0), stop=False,
                    )
            for e in range(2):
                for k in range(CHUNK // P):
                    at = (2 * k + e) * P
                    nc.tensor.matmul(
                        bank[:, at : at + P], lhsT=x_pair[e][:, k * P : (k + 1) * P], rhs=ident[:],
                        is_transpose=True, start=False, stop=(k == CHUNK // P - 1 and e == 1),
                    )
            nc.scalar.activation(
                z_turned[c][u][:].rearrange("m (k p e) -> m k p e", k=CHUNK // P, e=2),
                bank[:].rearrange("m (k e p) -> m k p e", k=CHUNK // P, e=2),
                ACT.Copy,
                scale=-1.0,
            )

        def turn_back(c, bank, rounded):
            for u in range(2):
                words = z_turned[c][u][:].bitcast(F32)
                for k in range(CHUNK // P):
                    at = (2 * k + u) * P
                    nc.tensor.transpose(bank[:, at : at + P], words[:, k * P : (k + 1) * P], ident[:])
            nc.scalar.copy(
                rounded.bitcast(F32).rearrange("p (k m u) -> p k m u", k=CHUNK // P, u=2),
                bank[:].rearrange("p (k u m) -> p k m u", k=CHUNK // P, u=2),
            )

        def quantize_z(b, first, count, rounded):
            cols = slice(first, first + count)
            nc.vector.quantize_mx(
                out=z_codes[b][:, cols].bitcast(FP8X4),
                scales=z_plane[b][:, cols],
                in_=rounded,
            )

        def score_passes(score_banks, unit_no, passes):
            half, t = divmod(unit_no, N_TILES)
            bank = score_banks[unit_no % SCORE_BANKS]
            rows = slice(t * P, (t + 1) * P)
            cols = slice(half * BANK, (half + 1) * BANK)
            for b in passes:
                nc.tensor.matmul_mx(
                    bank[:],
                    lhsT=wo_codes[b][:, rows].bitcast(FP8X4), lhsT_scale=wo_plane[b][:, rows],
                    rhs=z_codes[b][:, cols].bitcast(FP8X4), rhs_scale=z_plane[b][:, cols],
                    start=(b == 0), stop=(b == PASSES - 1),
                )

        def finish(score_banks, unit_no, result):
            half, t = divmod(unit_no, N_TILES)
            part = result[:, t * BANK : (t + 1) * BANK]
            nc.vector.tensor_tensor(part, score_banks[unit_no % SCORE_BANKS][:], part, ALU.subtract)
            nc.sync.dma_start(out[t * P : (t + 1) * P, half * BANK : (half + 1) * BANK], part)

        def load_target(half, tag):
            result = tile("result%d" % half, N_TILES * BANK, F32, tag=tag)
            nc.sync.dma_start(
                result[:].rearrange("p (t m) -> p t m", t=N_TILES),
                target.rearrange("(t p) m -> p t m", p=P)[:, :, half * BANK : (half + 1) * BANK],
            )
            return result

        warm_in = tile("warm_in", 8, F32, tag="staging")
        warm_out = tile("warm_out", 8, F32, tag="warm_then_wa")
        nc.gpsimd.memset(warm_in[:], 1.0)
        nc.gpsimd.memset(table_scales[:].bitcast(I32), 0)
        make_identity(nc, ident[:])
        nc.scalar.activation(warm_out[:, 0:1], warm_in[:, 0:1], ACT.Sqrt)
        nc.sync.dma_start(pick[:], offs)
        raw = load_wb(0, nc.sync, "z_then_x")
        nc.sync.dma_start(put[:], offs2)
        nc.sync.dma_start(read[:], offs3)
        load_scale_rows(nc.sync, table_scales, tab_scales)
        table = tile("table", T, U32, tag="staging")
        nc.sync.dma_start(table[:].bitcast(I32), tab_words[0].rearrange("p t i -> p (t i)").bitcast(I32))
        wa_codes = tile("wa_codes", 2 * H, U8, tag="warm_then_wa")
        nc.sync.dma_start(wa_codes[:].bitcast(I32), wa_words[0].bitcast(I32))
        for page in pages[:-1]:
            nc.vector.memset(page[:], 0.0)
        nc.vector.memset(wa_plane[:].bitcast(I32), 0)
        load_scale_rows(nc.sync, wa_plane, wa_scales)
        nc.vector.memset(pages[-1][:], 0.0)
        quantize_columns("wb0", raw, wb_codes[0], wb_plane[0], 0, PIECE, "rounded_then_unit", 1)
        quantize_columns("wb0", raw, wb_codes[0], wb_plane[0], PIECE, PIECE)
        unit_cols = tile("unit_cols", PASSES * PACK, F32, tag="rounded_then_unit")
        nc.sync.dma_start(
            unit_cols[:].rearrange("p (b i) -> p b i", i=PACK), unit.rearrange("(b p i) -> p b i", p=P, i=PACK)
        )
        for half in range(2):
            nc.vector.tensor_copy(v_scales[half][:], table_scales[:].indirect(pick[:, 32 * half : 32 * (half + 1)]))
            nc.vector.tensor_copy(v_words[half][:], table[:].indirect(pick[:, 32 * half : 32 * (half + 1)]))
        wgs_sb = tile("wgs_sb", S, F32, tag="scales_then_wgs")
        nc.sync.dma_start(wgs_sb[:], wgs)
        raw = load_wb(1, nc.sync, "staging")
        z_whole = tile("z_whole", PACK * M, BF16, tag="z_then_x")
        z_rounded = [z_whole[:, c * PACK * CHUNK : (c + 1) * PACK * CHUNK] for c in range(CHUNKS)]

        low, high = [0, 1, 2, 3], [4, 5, 6, 7]
        every = list(range(PACK))

        def z_pass(b, clay_sb, z_banks):
            for c in range(CHUNKS):
                for u in range(2):
                    x_pair = [x[:, c * CHUNK : (c + 1) * CHUNK] for x in x_neg[2 * u : 2 * u + 2]]
                    turn_pair(c, u, x_pair, clay_sb, z_banks[(3 * c + u) % len(z_banks)])
                turn_back(c, z_banks[(3 * c + 2) % len(z_banks)], z_rounded[c])
            quantize_z(b, 0, M, z_whole[:])

        for step, blocks in enumerate(([0], [1], [2], [3], [4, 5], [6, 7])):
            square_products(0, blocks)
            roots(0, blocks, every, 1 if step == 0 else PACK // len(blocks), True)
            if step == 3:
                quantize_columns("wb1", raw, wb_codes[1], wb_plane[1], 0, PIECE)
                quantize_columns("wb1", raw, wb_codes[1], wb_plane[1], PIECE, PIECE, "rounded_then_clay", 1)
                clay_sb = load_clay(0)
                raw = load_wb(2, nc.scalar, "staging")
            if step == 4:
                quantize_wb(2, raw, PIECE)
                wgt_raw = tile("wgt_raw", M, F32, tag="staging")
                nc.scalar.dma_start(wgt_raw[:], wgt)
        nc.scalar.mul(wgt_neg[:], wgt_raw[:], -1.0)
        raw = load_wo(0)
        for i in every:
            read_page(i, 0, x_neg[i])
        square_products(1, low)
        roots(1, low, every, 1, True)
        square_products(1, high)
        roots(1, high, every, 1, True)
        quantize_wo(0, raw)
        raw = load_wo(1)
        z_pass(0, clay_sb, last_taken(PACK))
        clay_sb = load_clay(1)
        for i in every:
            read_page(i, 0, x_neg[i])
        last = PACK - 1
        square_products(2, low)
        roots(2, low, every[:last], 1, True)
        held = [add_squares(low, [last])]
        free = [bank for bank in banks if bank is not held[0]]
        ring["banks"] = free
        quantize_wo(1, raw)
        raw = load_wo(2)
        square_products(2, high)
        roots(2, high, every[:last], 1, True)
        z_banks = last_taken(PACK)
        z_banks = z_banks[1:] + z_banks[:1]
        held.append(add_squares(high, [last]))
        quantize_wo(2, raw)
        results = [load_target(0, "squares_then_result"), load_target(1, "staging")]
        last_clay = load_last_clay()
        z_pass(1, clay_sb, z_banks)
        others = [bank for bank in free if bank is not held[1]]
        score_banks = others[:SCORE_BANKS]
        z_banks = held + others[SCORE_BANKS:]
        x_last = tile("x_last", PACK * M + S, F32, tag="z_then_x")
        x_neg = [x_last[:, i * M : (i + 1) * M] for i in every]
        h_last = x_last[:, PACK * M :]
        for i in range(2):
            read_page(i, 0, x_neg[i])
        for half in range(2):
            root(PASSES - 1, last, h_last[:, half * BANK : (half + 1) * BANK], held[half][:])
        put_columns(last, 0, h_last)
        for unit_no in range(SCORE_BANKS):
            score_passes(score_banks, unit_no, [0, 1])
        ring["banks"] = z_banks
        ring["at"] = 0

        def pair(c, u):
            return [x[:, c * CHUNK : (c + 1) * CHUNK] for x in x_neg[2 * u : 2 * u + 2]]

        for c in range(CHUNKS):
            turn_pair(c, 0, pair(c, 0), last_clay, take_bank())
        for half in range(2):
            z_half = tile("z_half%d" % half, PACK * BANK, BF16, tag="x_then_z%d" % half)
            for c in range(2 * half, 2 * half + 2):
                for e in range(2):
                    read_page(2 + e, c * CHUNK, pair(c, 1)[e])
                turn_pair(c, 1, pair(c, 1), last_clay, take_bank())
            for k in range(2):
                turn_back(2 * half + k, take_bank(), z_half[:, k * PACK * CHUNK : (k + 1) * PACK * CHUNK])
            quantize_z(2, half * BANK, BANK, z_half[:])
            if half == 1:
                for unit_no in range(SCORE_BANKS):
                    score_passes(score_banks, unit_no, [2])
        for unit_no in range(2 * N_TILES):
            if unit_no >= SCORE_BANKS:
                score_passes(score_banks, unit_no, [0, 1, 2])
            finish(score_banks, unit_no, results[unit_no // N_TILES])
